import numpy as np
import ml_dtypes


def mxq(x, axis, fmt="e4m3"):
    dtype, down = {"e4m3": (ml_dtypes.float8_e4m3fn, 7), "e5m2": (ml_dtypes.float8_e5m2, 14)}[fmt]
    v = np.moveaxis(np.asarray(x, np.float32).astype(ml_dtypes.bfloat16).astype(np.float64), axis, -1)
    blocks = v.reshape(v.shape[:-1] + (-1, 32))
    amax = np.abs(blocks).max(-1, keepdims=True)
    byte = np.maximum(np.where(amax > 0, np.frexp(amax)[1] - 1 + 127, 0) - down, 1)
    scale = np.exp2(byte - 127.0)
    codes = (blocks / scale).astype(np.float32).astype(dtype).astype(np.float64)
    return np.moveaxis((codes * scale).reshape(v.shape), -1, axis)


WIDE = False


def mx_kscale(k):
    if not WIDE:
        return np.ones(k)
    levels = np.array([10, -10, 5, -5, 0])
    if k % 512:
        return np.exp2(np.random.permutation(np.resize(levels, k // 32))).repeat(32)
    a = np.empty((k // 512, 16))
    for p in range(k // 512):
        a[p, :8] = np.random.permutation(np.resize(levels, 8))
        for g in range(8):
            far = levels[np.abs(levels - a[p, g]) >= 10]
            a[p, g + 8] = far[np.random.randint(len(far))]
    return np.exp2(a.ravel()).repeat(32)


def f64(x):
    return np.asarray(x).astype(np.float64)


def striped(idx):
    return np.tile(np.asarray(idx).reshape(-1, 16).T, (8, 1)).astype(np.uint16)


def unstriped(offs):
    return offs[:16].T.reshape(-1).astype(np.int64)


D, T, I, Q = 512, 1024, 512, 256


def setup_inputs():
    n = np.random.standard_normal
    idx = np.random.permutation(T // 2)[:I]
    idx2 = np.random.permutation(T // 2)[:I] + T // 2
    fd = mx_kscale(D)
    return {
        "query": (n((D, Q)) * 0.8 / np.sqrt(D) * fd[:, None]).astype(np.float32),
        "run": ((np.cumsum(np.round(n((D, T)) * 32) / 32, axis=1)) / fd[:, None]).astype(np.float32),
        "inv": (np.random.uniform(0.02, 0.08, (1, I))).astype(np.float32),
        "offs": striped(idx),
        "offs2": striped(idx2),
    }


def reference(query, run, inv, offs, offs2):
    idx = unstriped(offs)
    idx2 = unstriped(offs2)
    km = (f64(run)[:, idx2] - f64(run)[:, idx]) * f64(inv)
    queryq = mxq(f64(query), 0, "e4m3")
    kmq = mxq(km, 0, "e4m3")
    a = queryq.T @ kmq
    p = np.exp(a - np.max(a, axis=1, keepdims=True))
    y = p / np.sum(p, axis=1, keepdims=True) * 512.0
    return y

@@ -1,0 +1,172 @@
+from contextlib import ExitStack
+
+import concourse.mybir as mybir
+from concourse.masks import make_identity
+
+D, T, SPANS, ROWS = 512, 1024, 512, 256
+FLOPS = 2 * D * SPANS * ROWS
+
+F32 = mybir.dt.float32
+BF16 = mybir.dt.bfloat16
+U32 = mybir.dt.uint32
+U16 = mybir.dt.uint16
+U8 = mybir.dt.uint8
+FP8X4 = mybir.dt.float8_e4m3fn_x4
+ACT = mybir.ActivationFunctionType
+ALU = mybir.AluOpType
+
+P = 128
+PACK = 4
+HALF = T // 2
+CHUNKS = SPANS // P
+LIST_COLS = P // 16
+
+
+def tile_attend_spansums_kernel(tc, query, run, inv, offs, offs2, out):
+    nc = tc.nc
+    with ExitStack() as ctx:
+        lists = ctx.enter_context(tc.tile_pool(name="lists", bufs=1))
+        sb = ctx.enter_context(tc.tile_pool(name="sb", bufs=1))
+        ps = ctx.enter_context(tc.psum_pool(name="ps", bufs=1))
+
+        start_list = lists.tile([P, SPANS // 16], U16, name="start_list")
+        end_list = lists.tile([P, SPANS // 16], U16, name="end_list")
+        planes = [sb.tile([P, T], F32, name=f"plane{t}") for t in range(PACK)]
+        run_rows = run.rearrange("(p t) c -> t p c", t=PACK)
+        q_raw = sb.tile([P, PACK, ROWS], F32, name="q_raw")
+        inv_cols = sb.tile([P, CHUNKS], F32, name="inv_cols")
+
+        nc.sync.dma_start(start_list[:], offs)
+        nc.sync.dma_start(planes[0][:, 0:HALF], run_rows[0][:, 0:HALF])
+        nc.sync.dma_start(end_list[:], offs2)
+        nc.sync.dma_start(planes[0][:, HALF:T], run_rows[0][:, HALF:T])
+        with nc.allow_non_contiguous_dma(reason="one factor a partition"):
+            nc.sync.dma_start(inv_cols[:], inv.rearrange("o (c p) -> p (o c)", p=P))
+        nc.sync.dma_start(planes[1][:], run_rows[1])
+        nc.sync.dma_start(q_raw[:], query.rearrange("(p t) q -> p t q", t=PACK))
+        nc.sync.dma_start(planes[2][:], run_rows[2])
+        nc.sync.dma_start(planes[3][:], run_rows[3])
+
+        ident = sb.tile([P, P], F32, name="ident")
+        make_identity(nc, ident[:])
+        warm = sb.tile([P, 1], F32, name="warm")
+        nc.scalar.activation(warm[:], ident[:, 0:1], ACT.Exp)
+
+        def cols(c, n=1):
+            return slice(c * P, (c + n) * P)
+
+        def entries(c, n=1):
+            return slice(c * LIST_COLS, (c + n) * LIST_COLS)
+
+        turned = SPANS - P
+        starts = [sb.tile([P, turned], F32, name=f"starts{t}")[:] for t in range(PACK - 1)]
+        last_starts = sb.tile([P, SPANS], F32, name="last_starts")
+        starts = starts + [last_starts[:, 0:turned]]
+        direct_diffs = sb.tile([P, SPANS], F32, name="direct_diffs")
+        neg_starts = [sb.tile([P, turned], F32, name=f"neg_starts{t}") for t in range(PACK)]
+        ends = [sb.tile([P, turned], F32, name=f"ends{t}") for t in range(PACK)]
+
+        def turn(dst, src, start, stop):
+            nc.tensor.matmul(dst, src, ident[:], start=start, stop=stop, is_transpose=True)
+
+        inv_row = ps.tile([P, P], F32, name="inv_row", tag="bank7")
+        nc.tensor.transpose(inv_row[:], inv_cols[:, 0:1].to_broadcast([P, P]), ident[:])
+
+        diffs_t = [
+            [ps.tile([P, 2, 2, P], F32, name=f"diffs_t{u}_{b}", tag=f"bank{2 * u + b}") for b in range(2)]
+            for u in range(2)
+        ]
+        words = [ps.tile([P, 2, P], F32, name=f"words{c}", tag=f"bank{3 + c}") for c in range(1, CHUNKS)]
+        keys_t = [[sb.tile([P, P, 2], BF16, name=f"keys_t{c}_{u}") for u in range(2)] for c in range(1, CHUNKS)]
+        keys = [sb.tile([P, P, PACK], BF16, name=f"keys{c}", align_bytes=64) for c in range(CHUNKS)]
+        k_codes = [sb.tile([P, P], U32, name=f"k_codes{c}", align_bytes=64) for c in range(CHUNKS)]
+        k_scales = [sb.tile([P, P], U8, name=f"k_scales{c}", align_bytes=64) for c in range(CHUNKS)]
+        q_bf = sb.tile([P, ROWS, PACK], BF16, name="q_bf", align_bytes=64)
+
+        for t in range(PACK):
+            u, e = divmod(t, 2)
+            window = planes[t][:, 0:HALF] if t == 0 else planes[t][:]
+            nc.vector.tensor_copy(starts[t], window.indirect(start_list[:, entries(1, 3)]))
+            nc.scalar.mul(neg_starts[t][:], starts[t], -1.0)
+            nc.vector.tensor_copy(ends[t][:], planes[t][:].indirect(end_list[:, entries(1, 3)]))
+            for side, src in enumerate((neg_starts[t], ends[t])):
+                for c in range(1, CHUNKS):
+                    turn(
+                        diffs_t[u][c // 2][:, c % 2, e, :],
+                        src[:, cols(c - 1)],
+                        start=(e == 0 and side == 0 and c != 3),
+                        stop=(e == 1 and side == 1 and c != 2),
+                    )
+            if t == 1:
+                nc.scalar.copy(
+                    q_bf[:].rearrange("p (c i) t -> p c t i", i=4),
+                    q_raw[:].rearrange("p t (c i) -> p c t i", i=4),
+                )
+            if e == 1:
+                for c in range(1, CHUNKS):
+                    nc.scalar.activation(
+                        keys_t[c - 1][u][:],
+                        diffs_t[u][c // 2][:, c % 2].rearrange("i e p -> i p e"),
+                        ACT.Copy,
+                        scale=inv_cols[:, c : c + 1],
+                    )
+                    nc.tensor.transpose(
+                        words[c - 1][:, u, :],
+                        keys_t[c - 1][u][:].rearrange("i p e -> i (p e)").bitcast(F32),
+                        ident[:],
+                    )
+
+        for c in range(1, CHUNKS):
+            nc.scalar.copy(
+                keys[c][:].rearrange("p i t -> p (i t)").bitcast(F32).rearrange("p (i u) -> p i u", u=2),
+                words[c - 1][:].rearrange("p u i -> p i u"),
+            )
+
+        for t in range(PACK):
+            nc.vector.tensor_copy(last_starts[:, cols(t)], planes[t][:].indirect(start_list[:, entries(0)]))
+        for t in range(PACK):
+            nc.vector.tensor_tensor(
+                direct_diffs[:, cols(t)],
+                planes[t][:].indirect(end_list[:, entries(0)]),
+                last_starts[:, cols(t)],
+                ALU.subtract,
+            )
+        nc.vector.tensor_tensor(
+            keys[0][:].rearrange("p (c i) t -> p c t i", i=4),
+            direct_diffs[:].rearrange("p (t c i) -> p c t i", t=PACK, i=4),
+            inv_row[:].rearrange("p (c o i) -> p c o i", o=1, i=4).to_broadcast([P, P // 4, PACK, 4]),
+            ALU.mult,
+        )
+
+        q_codes = sb.tile([P, ROWS], U32, name="q_codes", align_bytes=64)
+        q_scales = sb.tile([P, ROWS], U8, name="q_scales", align_bytes=64)
+        nc.vector.quantize_mx(q_codes[:].bitcast(FP8X4), q_scales[:], q_bf[:].rearrange("p q t -> p (q t)"))
+
+        scores = [ps.tile([P, SPANS], F32, name=f"scores{h}", tag=f"bank{h}") for h in range(2)]
+        for c in range(CHUNKS):
+            nc.vector.quantize_mx(
+                k_codes[c][:].bitcast(FP8X4), k_scales[c][:], keys[c][:].rearrange("p i t -> p (i t)")
+            )
+            for h in range(2):
+                nc.tensor.matmul_mx(
+                    scores[h][:, cols(c)],
+                    lhsT=q_codes[:, cols(h)].bitcast(FP8X4),
+                    lhsT_scale=q_scales[:, cols(h)],
+                    rhs=k_codes[c][:].bitcast(FP8X4),
+                    rhs_scale=k_scales[c][:],
+                    start=True,
+                    stop=True,
+                )
+
+        neg_max = [sb.tile([P, 1], F32, name=f"neg_max{h}") for h in range(2)]
+        total = [sb.tile([P, 1], F32, name=f"total{h}") for h in range(2)]
+        recip = [sb.tile([P, 1], F32, name=f"recip{h}") for h in range(2)]
+        probs = [sb.tile([P, SPANS], F32, name=f"probs{h}") for h in range(2)]
+        result = [sb.tile([P, SPANS], F32, name=f"result{h}") for h in range(2)]
+        for h in range(2):
+            nc.vector.tensor_reduce(neg_max[h][:], scores[h][:], mybir.AxisListType.X, ALU.max, negate=True)
+            nc.scalar.activation(probs[h][:], scores[h][:], ACT.Exp, bias=neg_max[h][:], accum_out=total[h][:])
+        for h in range(2):
+            nc.vector.reciprocal(recip[h][:], total[h][:])
+            nc.vector.tensor_scalar(result[h][:], probs[h][:], recip[h][:], float(SPANS), ALU.mult, ALU.mult)
+            nc.sync.dma_start(out[cols(h), :], result[h][:])

@@ -31,21 +31,33 @@ def tile_attend_spansums_kernel(tc, query, run, inv, offs, offs2, out):
 
         start_list = lists.tile([P, SPANS // 16], U16, name="start_list")
         end_list = lists.tile([P, SPANS // 16], U16, name="end_list")
-        planes = [sb.tile([P, T], F32, name=f"plane{t}") for t in range(PACK)]
-        run_rows = run.rearrange("(p t) c -> t p c", t=PACK)
+        halves = sb.tile([P, 2 * PACK * HALF], F32, name="halves")
+        run_rows = run.rearrange("(p t) c -> p t c", t=PACK)
         q_raw = sb.tile([P, PACK, ROWS], F32, name="q_raw")
         inv_cols = sb.tile([P, CHUNKS], F32, name="inv_cols")
 
+        def start_window(t, width):
+            first = (PACK - 1 - t) * HALF
+            return halves[:, first : first + width]
+
+        def end_window(t):
+            first = (PACK - 1 + t) * HALF
+            return halves[:, first : first + T]
+
+        nc.sync.dma_start(start_window(0, HALF), run_rows[:, 0, 0:HALF])
         nc.sync.dma_start(start_list[:], offs)
-        nc.sync.dma_start(planes[0][:, 0:HALF], run_rows[0][:, 0:HALF])
+        nc.sync.dma_start(start_window(1, HALF), run_rows[:, 1, 0:HALF])
+        q_rows = query.rearrange("(p t) q -> p t q", t=PACK)
+        nc.sync.dma_start(q_raw[:, 0:2, :], q_rows[:, 0:2, :])
+        nc.sync.dma_start(q_raw[:, 2:PACK, :], q_rows[:, 2:PACK, :])
+        nc.sync.dma_start(start_window(2, HALF), run_rows[:, 2, 0:HALF])
+        nc.sync.dma_start(start_window(3, HALF), run_rows[:, 3, 0:HALF])
         nc.sync.dma_start(end_list[:], offs2)
-        nc.sync.dma_start(planes[0][:, HALF:T], run_rows[0][:, HALF:T])
+        nc.sync.dma_start(
+            halves[:, PACK * HALF :].rearrange("p (t c) -> p t c", t=PACK), run_rows[:, :, HALF:T]
+        )
         with nc.allow_non_contiguous_dma(reason="one factor a partition"):
             nc.sync.dma_start(inv_cols[:], inv.rearrange("o (c p) -> p (o c)", p=P))
-        nc.sync.dma_start(planes[1][:], run_rows[1])
-        nc.sync.dma_start(q_raw[:], query.rearrange("(p t) q -> p t q", t=PACK))
-        nc.sync.dma_start(planes[2][:], run_rows[2])
-        nc.sync.dma_start(planes[3][:], run_rows[3])
 
         ident = sb.tile([P, P], F32, name="ident")
         make_identity(nc, ident[:])
@@ -58,91 +70,70 @@ def tile_attend_spansums_kernel(tc, query, run, inv, offs, offs2, out):
         def entries(c, n=1):
             return slice(c * LIST_COLS, (c + n) * LIST_COLS)
 
-        turned = SPANS - P
-        starts = [sb.tile([P, turned], F32, name=f"starts{t}")[:] for t in range(PACK - 1)]
-        last_starts = sb.tile([P, SPANS], F32, name="last_starts")
-        starts = starts + [last_starts[:, 0:turned]]
-        direct_diffs = sb.tile([P, SPANS], F32, name="direct_diffs")
-        neg_starts = [sb.tile([P, turned], F32, name=f"neg_starts{t}") for t in range(PACK)]
-        ends = [sb.tile([P, turned], F32, name=f"ends{t}") for t in range(PACK)]
+        starts = [sb.tile([P, SPANS], F32, name=f"starts{t}") for t in range(PACK)]
+        neg_starts = [sb.tile([P, SPANS], F32, name=f"neg_starts{t}") for t in range(PACK)]
+        ends = [sb.tile([P, SPANS], F32, name=f"ends{t}", tag=f"ends{t}", align_bytes=64) for t in range(PACK)]
 
         def turn(dst, src, start, stop):
             nc.tensor.matmul(dst, src, ident[:], start=start, stop=stop, is_transpose=True)
 
-        inv_row = ps.tile([P, P], F32, name="inv_row", tag="bank7")
-        nc.tensor.transpose(inv_row[:], inv_cols[:, 0:1].to_broadcast([P, P]), ident[:])
-
-        diffs_t = [
-            [ps.tile([P, 2, 2, P], F32, name=f"diffs_t{u}_{b}", tag=f"bank{2 * u + b}") for b in range(2)]
-            for u in range(2)
-        ]
-        words = [ps.tile([P, 2, P], F32, name=f"words{c}", tag=f"bank{3 + c}") for c in range(1, CHUNKS)]
-        keys_t = [[sb.tile([P, P, 2], BF16, name=f"keys_t{c}_{u}") for u in range(2)] for c in range(1, CHUNKS)]
+        parts = [(c, 0, PACK) for c in range(CHUNKS - 1)] + [(CHUNKS - 1, 0, 2), (CHUNKS - 1, 2, 2)]
+        diffs_t = [ps.tile([P, n, P], F32, name=f"diffs_t{k}", tag=f"bank{k}") for k, (c, t0, n) in enumerate(parts)]
+        keys_t = [sb.tile([P, n // 2, P, 2], BF16, name=f"keys_t{k}") for k, (c, t0, n) in enumerate(parts)]
         keys = [sb.tile([P, P, PACK], BF16, name=f"keys{c}", align_bytes=64) for c in range(CHUNKS)]
         k_codes = [sb.tile([P, P], U32, name=f"k_codes{c}", align_bytes=64) for c in range(CHUNKS)]
         k_scales = [sb.tile([P, P], U8, name=f"k_scales{c}", align_bytes=64) for c in range(CHUNKS)]
         q_bf = sb.tile([P, ROWS, PACK], BF16, name="q_bf", align_bytes=64)
 
         for t in range(PACK):
-            u, e = divmod(t, 2)
-            window = planes[t][:, 0:HALF] if t == 0 else planes[t][:]
-            nc.vector.tensor_copy(starts[t], window.indirect(start_list[:, entries(1, 3)]))
-            nc.scalar.mul(neg_starts[t][:], starts[t], -1.0)
-            nc.vector.tensor_copy(ends[t][:], planes[t][:].indirect(end_list[:, entries(1, 3)]))
-            for side, src in enumerate((neg_starts[t], ends[t])):
-                for c in range(1, CHUNKS):
-                    turn(
-                        diffs_t[u][c // 2][:, c % 2, e, :],
-                        src[:, cols(c - 1)],
-                        start=(e == 0 and side == 0 and c != 3),
-                        stop=(e == 1 and side == 1 and c != 2),
+            if t == 0:
+                for c in (0, 2):
+                    nc.vector.tensor_copy(
+                        starts[t][:, cols(c, 2)], start_window(t, HALF).indirect(start_list[:, entries(c, 2)])
                     )
-            if t == 1:
-                nc.scalar.copy(
-                    q_bf[:].rearrange("p (c i) t -> p c t i", i=4),
-                    q_raw[:].rearrange("p t (c i) -> p c t i", i=4),
-                )
-            if e == 1:
-                for c in range(1, CHUNKS):
-                    nc.scalar.activation(
-                        keys_t[c - 1][u][:],
-                        diffs_t[u][c // 2][:, c % 2].rearrange("i e p -> i p e"),
-                        ACT.Copy,
-                        scale=inv_cols[:, c : c + 1],
-                    )
-                    nc.tensor.transpose(
-                        words[c - 1][:, u, :],
-                        keys_t[c - 1][u][:].rearrange("i p e -> i (p e)").bitcast(F32),
-                        ident[:],
-                    )
+            else:
+                nc.vector.tensor_copy(starts[t][:], start_window(t, T).indirect(start_list[:]))
+            nc.scalar.mul(neg_starts[t][:], starts[t][:], -1.0)
+            for k, (c, t0, n) in enumerate(parts):
+                if t0 <= t < t0 + n:
+                    turn(diffs_t[k][:, t - t0, :], neg_starts[t][:, cols(c)], start=(t == t0), stop=False)
 
-        for c in range(1, CHUNKS):
-            nc.scalar.copy(
-                keys[c][:].rearrange("p i t -> p (i t)").bitcast(F32).rearrange("p (i u) -> p i u", u=2),
-                words[c - 1][:].rearrange("p u i -> p i u"),
-            )
-
-        for t in range(PACK):
-            nc.vector.tensor_copy(last_starts[:, cols(t)], planes[t][:].indirect(start_list[:, entries(0)]))
-        for t in range(PACK):
-            nc.vector.tensor_tensor(
-                direct_diffs[:, cols(t)],
-                planes[t][:].indirect(end_list[:, entries(0)]),
-                last_starts[:, cols(t)],
-                ALU.subtract,
-            )
-        nc.vector.tensor_tensor(
-            keys[0][:].rearrange("p (c i) t -> p c t i", i=4),
-            direct_diffs[:].rearrange("p (t c i) -> p c t i", t=PACK, i=4),
-            inv_row[:].rearrange("p (c o i) -> p c o i", o=1, i=4).to_broadcast([P, P // 4, PACK, 4]),
-            ALU.mult,
+        nc.scalar.copy(
+            q_bf[:].rearrange("p (c i) t -> p c t i", i=4),
+            q_raw[:].rearrange("p t (c i) -> p c t i", i=4),
         )
-
-        q_codes = sb.tile([P, ROWS], U32, name="q_codes", align_bytes=64)
         q_scales = sb.tile([P, ROWS], U8, name="q_scales", align_bytes=64)
+
+        words = {}
+        for k, (c, t0, n) in enumerate(parts):
+            for t in range(t0, t0 + n):
+                nc.vector.tensor_copy(ends[t][:, cols(c)], end_window(t).indirect(end_list[:, entries(c)]))
+                turn(diffs_t[k][:, t - t0, :], ends[t][:, cols(c)], start=False, stop=(t == t0 + n - 1))
+            nc.scalar.activation(
+                keys_t[k][:],
+                diffs_t[k][:].rearrange("i (u e) p -> i u p e", e=2),
+                ACT.Copy,
+                scale=inv_cols[:, c : c + 1],
+            )
+            if t0 == 0:
+                words[c] = ps.tile([P, 2, P], F32, name=f"words{c}", tag=f"bank{5 + c % 3}")
+            for u in range(n // 2):
+                nc.tensor.transpose(
+                    words[c][:, t0 // 2 + u, :],
+                    keys_t[k][:, u].rearrange("i p e -> i (p e)").bitcast(F32),
+                    ident[:],
+                )
+            if t0 + n == PACK:
+                copy = nc.vector.tensor_copy if c == CHUNKS - 2 else nc.scalar.copy
+                copy(
+                    keys[c][:].rearrange("p i t -> p (i t)").bitcast(F32).rearrange("p (i u) -> p i u", u=2),
+                    words[c][:].rearrange("p u i -> p i u"),
+                )
+
+        q_codes = sb.tile([P, ROWS], U32, name="q_codes", tag="ends0", align_bytes=64)
         nc.vector.quantize_mx(q_codes[:].bitcast(FP8X4), q_scales[:], q_bf[:].rearrange("p q t -> p (q t)"))
 
-        scores = [ps.tile([P, SPANS], F32, name=f"scores{h}", tag=f"bank{h}") for h in range(2)]
+        scores = [ps.tile([P, SPANS], F32, name=f"scores{h}", tag=f"bank{(4, 7)[h]}") for h in range(2)]
         for c in range(CHUNKS):
             nc.vector.quantize_mx(
                 k_codes[c][:].bitcast(FP8X4), k_scales[c][:], keys[c][:].rearrange("p i t -> p (i t)")
@@ -168,5 +159,8 @@ def tile_attend_spansums_kernel(tc, query, run, inv, offs, offs2, out):
             nc.scalar.activation(probs[h][:], scores[h][:], ACT.Exp, bias=neg_max[h][:], accum_out=total[h][:])
         for h in range(2):
             nc.vector.reciprocal(recip[h][:], total[h][:])
-            nc.vector.tensor_scalar(result[h][:], probs[h][:], recip[h][:], float(SPANS), ALU.mult, ALU.mult)
-            nc.sync.dma_start(out[cols(h), :], result[h][:])
+            for part in (slice(0, SPANS),) if h == 0 else (cols(0, 2), cols(2, 2)):
+                nc.vector.tensor_scalar(
+                    result[h][:, part], probs[h][:, part], recip[h][:], float(SPANS), ALU.mult, ALU.mult
+                )
+                nc.sync.dma_start(out[cols(h), part], result[h][:, part])

@@ -47,20 +47,22 @@ def tile_attend_spansums_kernel(tc, query, run, inv, offs, offs2, out):
         nc.sync.dma_start(start_window(0, HALF), run_rows[:, 0, 0:HALF])
         nc.sync.dma_start(start_list[:], offs)
         nc.sync.dma_start(start_window(1, HALF), run_rows[:, 1, 0:HALF])
-        q_rows = query.rearrange("(p t) q -> p t q", t=PACK)
-        nc.sync.dma_start(q_raw[:, 0:2, :], q_rows[:, 0:2, :])
-        nc.sync.dma_start(q_raw[:, 2:PACK, :], q_rows[:, 2:PACK, :])
+        nc.sync.dma_start(end_list[:], offs2)
         nc.sync.dma_start(start_window(2, HALF), run_rows[:, 2, 0:HALF])
         nc.sync.dma_start(start_window(3, HALF), run_rows[:, 3, 0:HALF])
-        nc.sync.dma_start(end_list[:], offs2)
         nc.sync.dma_start(
             halves[:, PACK * HALF :].rearrange("p (t c) -> p t c", t=PACK), run_rows[:, :, HALF:T]
         )
-        with nc.allow_non_contiguous_dma(reason="one factor a partition"):
-            nc.sync.dma_start(inv_cols[:], inv.rearrange("o (c p) -> p (o c)", p=P))
+        nc.sync.dma_start(q_raw[:], query.rearrange("(p t) q -> p t q", t=PACK))
 
+        inv_rows = sb.tile([P, P], F32, name="inv_rows")
+        nc.gpsimd.memset(inv_rows[:], 0.0)
+        nc.scalar.dma_start(inv_rows[0:CHUNKS, :], inv.rearrange("o (c p) -> (o c) p", p=P))
         ident = sb.tile([P, P], F32, name="ident")
         make_identity(nc, ident[:])
+        inv_turned = ps.tile([P, P], F32, name="inv_turned", tag="bank5")
+        nc.tensor.transpose(inv_turned[:], inv_rows[:], ident[:])
+        nc.scalar.copy(inv_cols[:], inv_turned[:, 0:CHUNKS])
         warm = sb.tile([P, 1], F32, name="warm")
         nc.scalar.activation(warm[:], ident[:, 0:1], ACT.Exp)
 

@@ -109,7 +109,11 @@ def tile_attend_spansums_kernel(tc, query, run, inv, offs, offs2, out):
         words = {}
         for k, (c, t0, n) in enumerate(parts):
             for t in range(t0, t0 + n):
-                nc.vector.tensor_copy(ends[t][:, cols(c)], end_window(t).indirect(end_list[:, entries(c)]))
+                if c != 1:
+                    width = 2 if c == 0 else 1
+                    nc.vector.tensor_copy(
+                        ends[t][:, cols(c, width)], end_window(t).indirect(end_list[:, entries(c, width)])
+                    )
                 turn(diffs_t[k][:, t - t0, :], ends[t][:, cols(c)], start=False, stop=(t == t0 + n - 1))
             nc.scalar.activation(
                 keys_t[k][:],
@@ -126,7 +130,7 @@ def tile_attend_spansums_kernel(tc, query, run, inv, offs, offs2, out):
                     ident[:],
                 )
             if t0 + n == PACK:
-                copy = nc.vector.tensor_copy if c == CHUNKS - 2 else nc.scalar.copy
+                copy = nc.vector.tensor_copy if c in (1, 2) else nc.scalar.copy
                 copy(
                     keys[c][:].rearrange("p i t -> p (i t)").bitcast(F32).rearrange("p (i u) -> p i u", u=2),
                     words[c][:].rearrange("p u i -> p i u"),
@@ -165,4 +169,5 @@ def tile_attend_spansums_kernel(tc, query, run, inv, offs, offs2, out):
                 nc.vector.tensor_scalar(
                     result[h][:, part], probs[h][:, part], recip[h][:], float(SPANS), ALU.mult, ALU.mult
                 )
-                nc.sync.dma_start(out[cols(h), part], result[h][:, part])
+                queue = nc.scalar if part.start > 0 else nc.sync
+                queue.dma_start(out[cols(h), part], result[h][:, part])

@@ -63,8 +63,6 @@ def tile_attend_spansums_kernel(tc, query, run, inv, offs, offs2, out):
         inv_turned = ps.tile([P, P], F32, name="inv_turned", tag="bank5")
         nc.tensor.transpose(inv_turned[:], inv_rows[:], ident[:])
         nc.scalar.copy(inv_cols[:], inv_turned[:, 0:CHUNKS])
-        warm = sb.tile([P, 1], F32, name="warm")
-        nc.scalar.activation(warm[:], ident[:, 0:1], ACT.Exp)
 
         def cols(c, n=1):
             return slice(c * P, (c + n) * P)

from contextlib import ExitStack

import concourse.mybir as mybir
from concourse.masks import make_identity

D, T, SPANS, ROWS = 512, 1024, 512, 256
FLOPS = 2 * D * SPANS * ROWS

F32 = mybir.dt.float32
BF16 = mybir.dt.bfloat16
U32 = mybir.dt.uint32
U16 = mybir.dt.uint16
U8 = mybir.dt.uint8
FP8X4 = mybir.dt.float8_e4m3fn_x4
ACT = mybir.ActivationFunctionType
ALU = mybir.AluOpType

P = 128
PACK = 4
HALF = T // 2
CHUNKS = SPANS // P
LIST_COLS = P // 16


def tile_attend_spansums_kernel(tc, query, run, inv, offs, offs2, out):
    nc = tc.nc
    with ExitStack() as ctx:
        lists = ctx.enter_context(tc.tile_pool(name="lists", bufs=1))
        sb = ctx.enter_context(tc.tile_pool(name="sb", bufs=1))
        ps = ctx.enter_context(tc.psum_pool(name="ps", bufs=1))

        start_list = lists.tile([P, SPANS // 16], U16, name="start_list")
        end_list = lists.tile([P, SPANS // 16], U16, name="end_list")
        halves = sb.tile([P, 2 * PACK * HALF], F32, name="halves")
        run_rows = run.rearrange("(p t) c -> p t c", t=PACK)
        q_raw = sb.tile([P, PACK, ROWS], F32, name="q_raw")
        inv_cols = sb.tile([P, CHUNKS], F32, name="inv_cols")

        def start_window(t, width):
            first = (PACK - 1 - t) * HALF
            return halves[:, first : first + width]

        def end_window(t):
            first = (PACK - 1 + t) * HALF
            return halves[:, first : first + T]

        nc.sync.dma_start(start_window(0, HALF), run_rows[:, 0, 0:HALF])
        nc.sync.dma_start(start_list[:], offs)
        nc.sync.dma_start(start_window(1, HALF), run_rows[:, 1, 0:HALF])
        nc.sync.dma_start(end_list[:], offs2)
        nc.sync.dma_start(start_window(2, HALF), run_rows[:, 2, 0:HALF])
        nc.sync.dma_start(start_window(3, HALF), run_rows[:, 3, 0:HALF])
        nc.sync.dma_start(
            halves[:, PACK * HALF :].rearrange("p (t c) -> p t c", t=PACK), run_rows[:, :, HALF:T]
        )
        nc.sync.dma_start(q_raw[:], query.rearrange("(p t) q -> p t q", t=PACK))

        inv_rows = sb.tile([P, P], F32, name="inv_rows")
        nc.gpsimd.memset(inv_rows[:], 0.0)
        nc.scalar.dma_start(inv_rows[0:CHUNKS, :], inv.rearrange("o (c p) -> (o c) p", p=P))
        ident = sb.tile([P, P], F32, name="ident")
        make_identity(nc, ident[:])
        inv_turned = ps.tile([P, P], F32, name="inv_turned", tag="bank5")
        nc.tensor.transpose(inv_turned[:], inv_rows[:], ident[:])
        nc.scalar.copy(inv_cols[:], inv_turned[:, 0:CHUNKS])

        def cols(c, n=1):
            return slice(c * P, (c + n) * P)

        def entries(c, n=1):
            return slice(c * LIST_COLS, (c + n) * LIST_COLS)

        starts = [sb.tile([P, SPANS], F32, name=f"starts{t}") for t in range(PACK)]
        neg_starts = [sb.tile([P, SPANS], F32, name=f"neg_starts{t}") for t in range(PACK)]
        ends = [sb.tile([P, SPANS], F32, name=f"ends{t}", tag=f"ends{t}", align_bytes=64) for t in range(PACK)]

        def turn(dst, src, start, stop):
            nc.tensor.matmul(dst, src, ident[:], start=start, stop=stop, is_transpose=True)

        parts = [(c, 0, PACK) for c in range(CHUNKS - 1)] + [(CHUNKS - 1, 0, 2), (CHUNKS - 1, 2, 2)]
        diffs_t = [ps.tile([P, n, P], F32, name=f"diffs_t{k}", tag=f"bank{k}") for k, (c, t0, n) in enumerate(parts)]
        keys_t = [sb.tile([P, n // 2, P, 2], BF16, name=f"keys_t{k}") for k, (c, t0, n) in enumerate(parts)]
        keys = [sb.tile([P, P, PACK], BF16, name=f"keys{c}", align_bytes=64) for c in range(CHUNKS)]
        k_codes = [sb.tile([P, P], U32, name=f"k_codes{c}", align_bytes=64) for c in range(CHUNKS)]
        k_scales = [sb.tile([P, P], U8, name=f"k_scales{c}", align_bytes=64) for c in range(CHUNKS)]
        q_bf = sb.tile([P, ROWS, PACK], BF16, name="q_bf", align_bytes=64)

        for t in range(PACK):
            if t == 0:
                for c in (0, 2):
                    nc.vector.tensor_copy(
                        starts[t][:, cols(c, 2)], start_window(t, HALF).indirect(start_list[:, entries(c, 2)])
                    )
            else:
                nc.vector.tensor_copy(starts[t][:], start_window(t, T).indirect(start_list[:]))
            nc.scalar.mul(neg_starts[t][:], starts[t][:], -1.0)
            for k, (c, t0, n) in enumerate(parts):
                if t0 <= t < t0 + n:
                    turn(diffs_t[k][:, t - t0, :], neg_starts[t][:, cols(c)], start=(t == t0), stop=False)

        nc.scalar.copy(
            q_bf[:].rearrange("p (c i) t -> p c t i", i=4),
            q_raw[:].rearrange("p t (c i) -> p c t i", i=4),
        )
        q_scales = sb.tile([P, ROWS], U8, name="q_scales", align_bytes=64)

        words = {}
        for k, (c, t0, n) in enumerate(parts):
            for t in range(t0, t0 + n):
                if c != 1:
                    width = 2 if c == 0 else 1
                    nc.vector.tensor_copy(
                        ends[t][:, cols(c, width)], end_window(t).indirect(end_list[:, entries(c, width)])
                    )
                turn(diffs_t[k][:, t - t0, :], ends[t][:, cols(c)], start=False, stop=(t == t0 + n - 1))
            nc.scalar.activation(
                keys_t[k][:],
                diffs_t[k][:].rearrange("i (u e) p -> i u p e", e=2),
                ACT.Copy,
                scale=inv_cols[:, c : c + 1],
            )
            if t0 == 0:
                words[c] = ps.tile([P, 2, P], F32, name=f"words{c}", tag=f"bank{5 + c % 3}")
            for u in range(n // 2):
                nc.tensor.transpose(
                    words[c][:, t0 // 2 + u, :],
                    keys_t[k][:, u].rearrange("i p e -> i (p e)").bitcast(F32),
                    ident[:],
                )
            if t0 + n == PACK:
                copy = nc.vector.tensor_copy if c in (1, 2) else nc.scalar.copy
                copy(
                    keys[c][:].rearrange("p i t -> p (i t)").bitcast(F32).rearrange("p (i u) -> p i u", u=2),
                    words[c][:].rearrange("p u i -> p i u"),
                )

        q_codes = sb.tile([P, ROWS], U32, name="q_codes", tag="ends0", align_bytes=64)
        nc.vector.quantize_mx(q_codes[:].bitcast(FP8X4), q_scales[:], q_bf[:].rearrange("p q t -> p (q t)"))

        scores = [ps.tile([P, SPANS], F32, name=f"scores{h}", tag=f"bank{(4, 7)[h]}") for h in range(2)]
        for c in range(CHUNKS):
            nc.vector.quantize_mx(
                k_codes[c][:].bitcast(FP8X4), k_scales[c][:], keys[c][:].rearrange("p i t -> p (i t)")
            )
            for h in range(2):
                nc.tensor.matmul_mx(
                    scores[h][:, cols(c)],
                    lhsT=q_codes[:, cols(h)].bitcast(FP8X4),
                    lhsT_scale=q_scales[:, cols(h)],
                    rhs=k_codes[c][:].bitcast(FP8X4),
                    rhs_scale=k_scales[c][:],
                    start=True,
                    stop=True,
                )

        neg_max = [sb.tile([P, 1], F32, name=f"neg_max{h}") for h in range(2)]
        total = [sb.tile([P, 1], F32, name=f"total{h}") for h in range(2)]
        recip = [sb.tile([P, 1], F32, name=f"recip{h}") for h in range(2)]
        probs = [sb.tile([P, SPANS], F32, name=f"probs{h}") for h in range(2)]
        result = [sb.tile([P, SPANS], F32, name=f"result{h}") for h in range(2)]
        for h in range(2):
            nc.vector.tensor_reduce(neg_max[h][:], scores[h][:], mybir.AxisListType.X, ALU.max, negate=True)
            nc.scalar.activation(probs[h][:], scores[h][:], ACT.Exp, bias=neg_max[h][:], accum_out=total[h][:])
        for h in range(2):
            nc.vector.reciprocal(recip[h][:], total[h][:])
            for part in (slice(0, SPANS),) if h == 0 else (cols(0, 2), cols(2, 2)):
                nc.vector.tensor_scalar(
                    result[h][:, part], probs[h][:, part], recip[h][:], float(SPANS), ALU.mult, ALU.mult
                )
                queue = nc.scalar if part.start > 0 else nc.sync
                queue.dma_start(out[cols(h), part], result[h][:, part])
